import numpy as np
import ml_dtypes


def mxq(x, axis, fmt="e4m3"):
    dtype, down = {"e4m3": (ml_dtypes.float8_e4m3fn, 7), "e5m2": (ml_dtypes.float8_e5m2, 14)}[fmt]
    v = np.moveaxis(np.asarray(x, np.float32).astype(ml_dtypes.bfloat16).astype(np.float64), axis, -1)
    blocks = v.reshape(v.shape[:-1] + (-1, 32))
    amax = np.abs(blocks).max(-1, keepdims=True)
    byte = np.maximum(np.where(amax > 0, np.frexp(amax)[1] - 1 + 127, 0) - down, 1)
    scale = np.exp2(byte - 127.0)
    codes = (blocks / scale).astype(np.float32).astype(dtype).astype(np.float64)
    return np.moveaxis((codes * scale).reshape(v.shape), -1, axis)


WIDE = False


def mx_kscale(k):
    if not WIDE:
        return np.ones(k)
    levels = np.array([10, -10, 5, -5, 0])
    if k % 512:
        return np.exp2(np.random.permutation(np.resize(levels, k // 32))).repeat(32)
    a = np.empty((k // 512, 16))
    for p in range(k // 512):
        a[p, :8] = np.random.permutation(np.resize(levels, 8))
        for g in range(8):
            far = levels[np.abs(levels - a[p, g]) >= 10]
            a[p, g + 8] = far[np.random.randint(len(far))]
    return np.exp2(a.ravel()).repeat(32)


def f64(x):
    return np.asarray(x).astype(np.float64)


def striped8(idx):
    return np.asarray(idx).reshape(8, -1, 16).transpose(0, 2, 1).reshape(128, -1).astype(np.uint16)


def unstriped8(offs):
    return offs.reshape(8, 16, -1).transpose(0, 2, 1).reshape(8, -1).astype(np.int64)


def pick8(x, idx, run):
    r = np.arange(len(x))
    return x[r[:, None], idx[r % (8 * run) // run]]


E2M1 = np.array([0.0, 0.5, 1.0, 1.5, 2.0, 3.0, 4.0, 6.0, -0.0, -0.5, -1.0, -1.5, -2.0, -3.0, -4.0, -6.0])


def pack_weight(w, fmt):
    k, n = w.shape
    w = f64(np.asarray(w, np.float32).astype(ml_dtypes.bfloat16)).reshape(k // 32, 32, n)
    amax = np.abs(w).max(1)
    if fmt == "e4m3":
        byte = np.frexp(amax)[1] - 1 + 127 - 7
    else:
        mant, ex = np.frexp(amax / 6.0)
        byte = np.where(mant > 0.5, ex, ex - 1) + 127
    byte = np.clip(np.where(amax > 0, byte, 1), 1, 254)
    scaled = (w * np.exp2(127.0 - byte)[:, None, :]).reshape(k, n).astype(np.float32)
    by_word = np.ascontiguousarray(scaled.reshape(k // 512, 128, 4, n).transpose(0, 1, 3, 2))
    if fmt == "e4m3":
        words = by_word.astype(ml_dtypes.float8_e4m3fn).view(np.uint8)
    else:
        c = by_word.astype(ml_dtypes.float4_e2m1fn).view(np.uint8) & 0xF
        words = (c[..., 0::2] | (c[..., 1::2] << 4)).reshape(k // 512, 128, 2 * n)
    return np.ascontiguousarray(words), np.ascontiguousarray(byte.astype(np.uint8).reshape(k // 512, 16, n))


def unpack_weight(words, scales, fmt):
    g, _, n = scales.shape
    words = np.ascontiguousarray(words).reshape(g, 128, n, -1)
    if fmt == "e4m3":
        vals = words.view(ml_dtypes.float8_e4m3fn).astype(np.float64)
    else:
        nib = np.empty((g, 128, n, 4), np.uint8)
        nib[..., 0::2] = words & 0xF
        nib[..., 1::2] = words >> 4
        vals = E2M1[nib]
    vals = vals * np.repeat(np.exp2(scales.astype(np.float64) - 127.0), 8, axis=1)[..., None]
    return vals.transpose(0, 1, 3, 2).reshape(g * 512, n)


D, T, U, I, Q = 512, 1024, 1024, 512, 128


def setup_inputs():
    n = np.random.standard_normal
    idx = np.stack([np.random.permutation(T)[:I] for _ in range(8)])
    idx2 = np.stack([np.random.permutation(U)[:I] for _ in range(8)])
    idx3 = np.stack([np.random.permutation(T)[:I] for _ in range(8)])
    fd = mx_kscale(D)
    keysp = pack_weight(n((D, T)) / fd[:, None], "e2m1")
    notesp = pack_weight(n((D, U)) / fd[:, None], "e4m3")
    return {
        "query": (n((D, Q)) * 1.0 / np.sqrt(D) * fd[:, None]).astype(np.float32),
        "keys_words": keysp[0],
        "keys_scales": keysp[1],
        "notes_words": notesp[0],
        "notes_scales": notesp[1],
        "offs": striped8(idx),
        "offs2": striped8(idx2),
        "offs3": striped8(idx3),
    }


def reference(query, keys_words, keys_scales, notes_words, notes_scales, offs, offs2, offs3):
    idx = unstriped8(offs)
    idx2 = unstriped8(offs2)
    idx3 = unstriped8(offs3)
    keysu = unpack_weight(keys_words, keys_scales, "e2m1")
    notesu = unpack_weight(notes_words, notes_scales, "e4m3")
    queryq = mxq(f64(query), 0, "e4m3")
    a = queryq.T @ keysu
    b = queryq.T @ notesu
    r = pick8(b, idx2, 16) - pick8(a, idx, 16)
    f1 = np.zeros((Q, T))
    f1[np.arange(Q)[:, None], idx[np.arange(Q) % 128 // 16]] = r
    a2 = a + f1
    ta2 = np.max(a2, axis=1, keepdims=True)
    y = np.exp(pick8(a2, idx3, 16) - ta2)
    return y

@@ -1,0 +1,140 @@
+from contextlib import ExitStack
+
+import concourse.mybir as mybir
+
+D, T, U, I, Q = 512, 1024, 1024, 512, 128
+FLOPS = 2 * D * Q * (T + U)
+
+F32 = mybir.dt.float32
+BF16 = mybir.dt.bfloat16
+I32 = mybir.dt.int32
+U32 = mybir.dt.uint32
+U16 = mybir.dt.uint16
+U8 = mybir.dt.uint8
+FP8X4 = mybir.dt.float8_e4m3fn_x4
+FP4X4 = mybir.dt.float4_e2m1fn_x4
+ALU = mybir.AluOpType
+ACT = mybir.ActivationFunctionType
+AX = mybir.AxisListType
+
+P = 128
+PACK = 4
+LIST_COLS = I // 16
+HALF = I // 2
+HALF_COLS = LIST_COLS // 2
+
+
+def tile_attend_finerscores_two_kernel(
+    tc, query, keys_words, keys_scales, notes_words, notes_scales, offs, offs2, offs3, out
+):
+    nc = tc.nc
+    with ExitStack() as ctx:
+        keep = ctx.enter_context(tc.tile_pool(name="keep", bufs=1))
+        psum = ctx.enter_context(tc.psum_pool(name="psum", bufs=1))
+
+        token_list = keep.tile([P, LIST_COLS], U16, name="token_list")
+        note_list = keep.tile([P, LIST_COLS], U16, name="note_list")
+        out_list = keep.tile([P, LIST_COLS], U16, name="out_list")
+        q_raw = keep.tile([P, PACK, Q], F32, name="q_raw")
+        key_words = keep.tile([P, 2 * T], U8, name="key_words", align_bytes=64)
+        key_plane = keep.tile([P, T], U8, name="key_plane", align_bytes=64)
+        note_words = keep.tile([P, U], U32, name="note_words", align_bytes=64)
+        note_plane = keep.tile([P, U], U8, name="note_plane", align_bytes=64)
+
+        nc.sync.dma_start(out=q_raw[:], in_=query.rearrange("(p j) q -> p j q", j=PACK))
+        for r in range(4):
+            nc.scalar.dma_start(
+                out=key_plane[r:P:32, :].bitcast(I32), in_=keys_scales[0, r:16:4, :].bitcast(I32)
+            )
+        nc.sync.dma_start(out=key_words[:].bitcast(I32), in_=keys_words[0].bitcast(I32))
+        nc.sync.dma_start(
+            out=note_words[:].bitcast(I32),
+            in_=notes_words[0].rearrange("p n t -> p (n t)").bitcast(I32),
+        )
+        for r in range(4):
+            nc.sync.dma_start(
+                out=note_plane[r:P:32, :].bitcast(I32), in_=notes_scales[0, r:16:4, :].bitcast(I32)
+            )
+        nc.sync.dma_start(token_list[:], offs)
+        nc.sync.dma_start(note_list[:], offs2)
+        nc.sync.dma_start(out_list[:], offs3)
+
+        change = keep.tile([P, T], F32, name="change")
+        nc.vector.memset(change[:], 0.0)
+
+        q_grouped = keep.tile([P, Q, PACK], BF16, name="q_grouped", align_bytes=64)
+        nc.vector.tensor_copy(out=q_grouped[:], in_=q_raw[:].rearrange("p j q -> p q j"))
+        q_codes = keep.tile([P, Q], U32, name="q_codes", align_bytes=64)
+        q_plane = keep.tile([P, Q], U8, name="q_plane", align_bytes=64)
+        nc.vector.quantize_mx(
+            out=q_codes[:].bitcast(FP8X4),
+            scales=q_plane[:],
+            in_=q_grouped[:].rearrange("p q j -> p (q j)"),
+        )
+
+        def score(name, words, plane, width):
+            bank = psum.tile([P, width], F32, name=name)
+            nc.tensor.matmul_mx(
+                out=bank[:],
+                lhsT=q_codes[:].bitcast(FP8X4),
+                lhsT_scale=q_plane[:],
+                rhs=words,
+                rhs_scale=plane,
+                start=True,
+                stop=True,
+            )
+            return bank
+
+        a = keep.tile([P, T], F32, name="a")
+        b = keep.tile([P, U], F32, name="b")
+        a_banks = []
+        for c in range(2):
+            lo, hi = 512 * c, 512 * (c + 1)
+            bank = score("a_bank%d" % c, key_words[:, 2 * lo : 2 * hi].bitcast(FP4X4), key_plane[:, lo:hi], 512)
+            a_banks.append(bank)
+            if c == 0:
+                nc.vector.tensor_copy(out=a[:, lo:hi], in_=bank[:])
+            else:
+                nc.scalar.copy(out=a[:, lo:hi], in_=bank[:])
+        for c in range(4):
+            lo, hi = 256 * c, 256 * (c + 1)
+            bank = score("b_bank%d" % c, note_words[:, lo:hi].bitcast(FP8X4), note_plane[:, lo:hi], 256)
+            if c == 0:
+                nc.vector.tensor_copy(out=b[:, lo:hi], in_=bank[:])
+            else:
+                nc.scalar.copy(out=b[:, lo:hi], in_=bank[:])
+
+        minus_old = keep.tile([P, I], F32, name="minus_old")
+        nc.vector.tensor_scalar(
+            out=minus_old[:],
+            in0=a[:].indirect(token_list[:]),
+            scalar1=-1.0,
+            scalar2=0.0,
+            op0=ALU.mult,
+            op1=ALU.add,
+        )
+        for h in range(2):
+            cols = slice(h * HALF_COLS, (h + 1) * HALF_COLS)
+            slots = slice(h * HALF, (h + 1) * HALF)
+            new = keep.tile([P, HALF], F32, name="new%d" % h)
+            nc.scalar.activation(out=new[:], in_=b[:].indirect(note_list[:, cols]), func=ACT.Copy)
+            nc.vector.tensor_tensor(
+                out=change[:].indirect(token_list[:, cols]),
+                in0=new[:],
+                in1=minus_old[:, slots],
+                op=ALU.add,
+            )
+
+        a2 = keep.tile([P, T], F32, name="a2")
+        nc.vector.tensor_tensor(out=a2[:], in0=a[:], in1=change[:], op=ALU.add)
+        minus_top = keep.tile([P, 1], F32, name="minus_top")
+        nc.vector.tensor_reduce(out=minus_top[:], in_=a2[:], axis=AX.X, op=ALU.max, negate=True)
+
+        for h in range(2):
+            cols = slice(h * HALF_COLS, (h + 1) * HALF_COLS)
+            slots = slice(h * HALF, (h + 1) * HALF)
+            result = keep.tile([P, HALF], F32, name="result%d" % h)
+            nc.scalar.activation(
+                out=result[:], in_=a2[:].indirect(out_list[:, cols]), func=ACT.Exp, bias=minus_top[:]
+            )
+            nc.sync.dma_start(out=out[:, slots], in_=result[:])

@@ -43,7 +43,7 @@ def tile_attend_finerscores_two_kernel(
 
         nc.sync.dma_start(out=q_raw[:], in_=query.rearrange("(p j) q -> p j q", j=PACK))
         for r in range(4):
-            nc.scalar.dma_start(
+            nc.sync.dma_start(
                 out=key_plane[r:P:32, :].bitcast(I32), in_=keys_scales[0, r:16:4, :].bitcast(I32)
             )
         nc.sync.dma_start(out=key_words[:].bitcast(I32), in_=keys_words[0].bitcast(I32))
@@ -63,14 +63,19 @@ def tile_attend_finerscores_two_kernel(
         nc.vector.memset(change[:], 0.0)
 
         q_grouped = keep.tile([P, Q, PACK], BF16, name="q_grouped", align_bytes=64)
-        nc.vector.tensor_copy(out=q_grouped[:], in_=q_raw[:].rearrange("p j q -> p q j"))
         q_codes = keep.tile([P, Q], U32, name="q_codes", align_bytes=64)
         q_plane = keep.tile([P, Q], U8, name="q_plane", align_bytes=64)
-        nc.vector.quantize_mx(
-            out=q_codes[:].bitcast(FP8X4),
-            scales=q_plane[:],
-            in_=q_grouped[:].rearrange("p q j -> p (q j)"),
-        )
+        q_halves = [slice(0, Q // 2), slice(Q // 2, Q)]
+        for rows in q_halves:
+            nc.vector.tensor_copy(
+                out=q_grouped[:, rows, :], in_=q_raw[:, :, rows].rearrange("p j q -> p q j")
+            )
+        for rows in q_halves:
+            nc.vector.quantize_mx(
+                out=q_codes[:, rows].bitcast(FP8X4),
+                scales=q_plane[:, rows],
+                in_=q_grouped[:, rows, :].rearrange("p q j -> p (q j)"),
+            )
 
         def score(name, words, plane, width):
             bank = psum.tile([P, width], F32, name=name)
@@ -87,23 +92,13 @@ def tile_attend_finerscores_two_kernel(
 
         a = keep.tile([P, T], F32, name="a")
         b = keep.tile([P, U], F32, name="b")
-        a_banks = []
-        for c in range(2):
-            lo, hi = 512 * c, 512 * (c + 1)
-            bank = score("a_bank%d" % c, key_words[:, 2 * lo : 2 * hi].bitcast(FP4X4), key_plane[:, lo:hi], 512)
-            a_banks.append(bank)
-            if c == 0:
+        for c in range(4):
+            lo, hi = 256 * c, 256 * (c + 1)
+            bank = score("a_bank%d" % c, key_words[:, 2 * lo : 2 * hi].bitcast(FP4X4), key_plane[:, lo:hi], 256)
+            if c % 2 == 0:
                 nc.vector.tensor_copy(out=a[:, lo:hi], in_=bank[:])
             else:
                 nc.scalar.copy(out=a[:, lo:hi], in_=bank[:])
-        for c in range(4):
-            lo, hi = 256 * c, 256 * (c + 1)
-            bank = score("b_bank%d" % c, note_words[:, lo:hi].bitcast(FP8X4), note_plane[:, lo:hi], 256)
-            if c == 0:
-                nc.vector.tensor_copy(out=b[:, lo:hi], in_=bank[:])
-            else:
-                nc.scalar.copy(out=b[:, lo:hi], in_=bank[:])
-
         minus_old = keep.tile([P, I], F32, name="minus_old")
         nc.vector.tensor_scalar(
             out=minus_old[:],
@@ -113,17 +108,17 @@ def tile_attend_finerscores_two_kernel(
             op0=ALU.mult,
             op1=ALU.add,
         )
-        for h in range(2):
-            cols = slice(h * HALF_COLS, (h + 1) * HALF_COLS)
-            slots = slice(h * HALF, (h + 1) * HALF)
-            new = keep.tile([P, HALF], F32, name="new%d" % h)
-            nc.scalar.activation(out=new[:], in_=b[:].indirect(note_list[:, cols]), func=ACT.Copy)
-            nc.vector.tensor_tensor(
-                out=change[:].indirect(token_list[:, cols]),
-                in0=new[:],
-                in1=minus_old[:, slots],
-                op=ALU.add,
-            )
+        for c in range(4):
+            lo, hi = 256 * c, 256 * (c + 1)
+            bank = score("b_bank%d" % c, note_words[:, lo:hi].bitcast(FP8X4), note_plane[:, lo:hi], 256)
+            nc.scalar.copy(out=b[:, lo:hi], in_=bank[:])
+
+        new = keep.tile([P, I], F32, name="new")
+        nc.scalar.activation(out=new[:, :HALF], in_=b[:].indirect(note_list[:, :HALF_COLS]), func=ACT.Copy)
+        nc.vector.tensor_copy(out=new[:, HALF:], in_=b[:].indirect(note_list[:, HALF_COLS:]))
+        nc.vector.tensor_tensor(
+            out=change[:].indirect(token_list[:]), in0=new[:], in1=minus_old[:], op=ALU.add
+        )
 
         a2 = keep.tile([P, T], F32, name="a2")
         nc.vector.tensor_tensor(out=a2[:], in0=a[:], in1=change[:], op=ALU.add)

from contextlib import ExitStack

import concourse.mybir as mybir

D, T, U, I, Q = 512, 1024, 1024, 512, 128
FLOPS = 2 * D * Q * (T + U)

F32 = mybir.dt.float32
BF16 = mybir.dt.bfloat16
I32 = mybir.dt.int32
U32 = mybir.dt.uint32
U16 = mybir.dt.uint16
U8 = mybir.dt.uint8
FP8X4 = mybir.dt.float8_e4m3fn_x4
FP4X4 = mybir.dt.float4_e2m1fn_x4
ALU = mybir.AluOpType
ACT = mybir.ActivationFunctionType
AX = mybir.AxisListType

P = 128
PACK = 4
LIST_COLS = I // 16
HALF = I // 2
HALF_COLS = LIST_COLS // 2


def tile_attend_finerscores_two_kernel(
    tc, query, keys_words, keys_scales, notes_words, notes_scales, offs, offs2, offs3, out
):
    nc = tc.nc
    with ExitStack() as ctx:
        keep = ctx.enter_context(tc.tile_pool(name="keep", bufs=1))
        psum = ctx.enter_context(tc.psum_pool(name="psum", bufs=1))

        token_list = keep.tile([P, LIST_COLS], U16, name="token_list")
        note_list = keep.tile([P, LIST_COLS], U16, name="note_list")
        out_list = keep.tile([P, LIST_COLS], U16, name="out_list")
        q_raw = keep.tile([P, PACK, Q], F32, name="q_raw")
        key_words = keep.tile([P, 2 * T], U8, name="key_words", align_bytes=64)
        key_plane = keep.tile([P, T], U8, name="key_plane", align_bytes=64)
        note_words = keep.tile([P, U], U32, name="note_words", align_bytes=64)
        note_plane = keep.tile([P, U], U8, name="note_plane", align_bytes=64)

        nc.sync.dma_start(out=q_raw[:], in_=query.rearrange("(p j) q -> p j q", j=PACK))
        for r in range(4):
            nc.sync.dma_start(
                out=key_plane[r:P:32, :].bitcast(I32), in_=keys_scales[0, r:16:4, :].bitcast(I32)
            )
        nc.sync.dma_start(out=key_words[:].bitcast(I32), in_=keys_words[0].bitcast(I32))
        nc.sync.dma_start(
            out=note_words[:].bitcast(I32),
            in_=notes_words[0].rearrange("p n t -> p (n t)").bitcast(I32),
        )
        for r in range(4):
            nc.sync.dma_start(
                out=note_plane[r:P:32, :].bitcast(I32), in_=notes_scales[0, r:16:4, :].bitcast(I32)
            )
        nc.sync.dma_start(token_list[:], offs)
        nc.sync.dma_start(note_list[:], offs2)
        nc.sync.dma_start(out_list[:], offs3)

        change = keep.tile([P, T], F32, name="change")
        nc.vector.memset(change[:], 0.0)

        q_grouped = keep.tile([P, Q, PACK], BF16, name="q_grouped", align_bytes=64)
        q_codes = keep.tile([P, Q], U32, name="q_codes", align_bytes=64)
        q_plane = keep.tile([P, Q], U8, name="q_plane", align_bytes=64)
        q_halves = [slice(0, Q // 2), slice(Q // 2, Q)]
        for rows in q_halves:
            nc.vector.tensor_copy(
                out=q_grouped[:, rows, :], in_=q_raw[:, :, rows].rearrange("p j q -> p q j")
            )
        for rows in q_halves:
            nc.vector.quantize_mx(
                out=q_codes[:, rows].bitcast(FP8X4),
                scales=q_plane[:, rows],
                in_=q_grouped[:, rows, :].rearrange("p q j -> p (q j)"),
            )

        def score(name, words, plane, width):
            bank = psum.tile([P, width], F32, name=name)
            nc.tensor.matmul_mx(
                out=bank[:],
                lhsT=q_codes[:].bitcast(FP8X4),
                lhsT_scale=q_plane[:],
                rhs=words,
                rhs_scale=plane,
                start=True,
                stop=True,
            )
            return bank

        a = keep.tile([P, T], F32, name="a")
        b = keep.tile([P, U], F32, name="b")
        for c in range(4):
            lo, hi = 256 * c, 256 * (c + 1)
            bank = score("a_bank%d" % c, key_words[:, 2 * lo : 2 * hi].bitcast(FP4X4), key_plane[:, lo:hi], 256)
            if c % 2 == 0:
                nc.vector.tensor_copy(out=a[:, lo:hi], in_=bank[:])
            else:
                nc.scalar.copy(out=a[:, lo:hi], in_=bank[:])
        minus_old = keep.tile([P, I], F32, name="minus_old")
        nc.vector.tensor_scalar(
            out=minus_old[:],
            in0=a[:].indirect(token_list[:]),
            scalar1=-1.0,
            scalar2=0.0,
            op0=ALU.mult,
            op1=ALU.add,
        )
        for c in range(4):
            lo, hi = 256 * c, 256 * (c + 1)
            bank = score("b_bank%d" % c, note_words[:, lo:hi].bitcast(FP8X4), note_plane[:, lo:hi], 256)
            nc.scalar.copy(out=b[:, lo:hi], in_=bank[:])

        new = keep.tile([P, I], F32, name="new")
        nc.scalar.activation(out=new[:, :HALF], in_=b[:].indirect(note_list[:, :HALF_COLS]), func=ACT.Copy)
        nc.vector.tensor_copy(out=new[:, HALF:], in_=b[:].indirect(note_list[:, HALF_COLS:]))
        nc.vector.tensor_tensor(
            out=change[:].indirect(token_list[:]), in0=new[:], in1=minus_old[:], op=ALU.add
        )

        a2 = keep.tile([P, T], F32, name="a2")
        nc.vector.tensor_tensor(out=a2[:], in0=a[:], in1=change[:], op=ALU.add)
        minus_top = keep.tile([P, 1], F32, name="minus_top")
        nc.vector.tensor_reduce(out=minus_top[:], in_=a2[:], axis=AX.X, op=ALU.max, negate=True)

        for h in range(2):
            cols = slice(h * HALF_COLS, (h + 1) * HALF_COLS)
            slots = slice(h * HALF, (h + 1) * HALF)
            result = keep.tile([P, HALF], F32, name="result%d" % h)
            nc.scalar.activation(
                out=result[:], in_=a2[:].indirect(out_list[:, cols]), func=ACT.Exp, bias=minus_top[:]
            )
            nc.sync.dma_start(out=out[:, slots], in_=result[:])
